import numpy as np
import ml_dtypes


def mxq(x, axis, fmt="e4m3"):
    dtype, down = {"e4m3": (ml_dtypes.float8_e4m3fn, 7), "e5m2": (ml_dtypes.float8_e5m2, 14)}[fmt]
    v = np.moveaxis(np.asarray(x, np.float32).astype(ml_dtypes.bfloat16).astype(np.float64), axis, -1)
    blocks = v.reshape(v.shape[:-1] + (-1, 32))
    amax = np.abs(blocks).max(-1, keepdims=True)
    byte = np.maximum(np.where(amax > 0, np.frexp(amax)[1] - 1 + 127, 0) - down, 1)
    scale = np.exp2(byte - 127.0)
    codes = (blocks / scale).astype(np.float32).astype(dtype).astype(np.float64)
    return np.moveaxis((codes * scale).reshape(v.shape), -1, axis)


WIDE = False


def mx_kscale(k):
    if not WIDE:
        return np.ones(k)
    levels = np.array([10, -10, 5, -5, 0])
    if k % 512:
        return np.exp2(np.random.permutation(np.resize(levels, k // 32))).repeat(32)
    a = np.empty((k // 512, 16))
    for p in range(k // 512):
        a[p, :8] = np.random.permutation(np.resize(levels, 8))
        for g in range(8):
            far = levels[np.abs(levels - a[p, g]) >= 10]
            a[p, g + 8] = far[np.random.randint(len(far))]
    return np.exp2(a.ravel()).repeat(32)


def f64(x):
    return np.asarray(x).astype(np.float64)


def striped(idx):
    return np.tile(idx.reshape(-1, 16).T, (8, 1)).astype(np.uint16)


def unstriped(offs):
    return offs[:16].T.reshape(-1).astype(np.int64)


def striped8(idx):
    return np.concatenate([x.reshape(-1, 16).T for x in idx]).astype(np.uint16)


def runs(offs, k):
    lists = np.stack([offs[16 * r : 16 * r + 16].T.reshape(-1) for r in range(8)]).astype(np.int64)
    return lists[np.arange(k) % 512 // 64]


def pack_weight(w):
    k, n = w.shape
    w = f64(np.asarray(w, np.float32).astype(ml_dtypes.bfloat16)).reshape(k // 32, 32, n)
    amax = np.abs(w).max(1)
    byte = np.clip(np.where(amax > 0, np.frexp(amax)[1] - 1 + 127 - 7, 1), 1, 254)
    scaled = (w * np.exp2(127.0 - byte)[:, None, :]).reshape(k, n).astype(np.float32)
    words = np.ascontiguousarray(scaled.reshape(k // 512, 128, 4, n).transpose(0, 1, 3, 2)).astype(ml_dtypes.float8_e4m3fn).view(np.uint8)
    return words, np.ascontiguousarray(byte.astype(np.uint8).reshape(k // 512, 16, n))


def unpack_weight(words, scales):
    g, p, n, _ = words.shape
    vals = np.ascontiguousarray(words).view(ml_dtypes.float8_e4m3fn).astype(np.float64) * np.repeat(np.exp2(scales.astype(np.float64) - 127.0), 8, axis=1)[..., None]
    return vals.transpose(0, 1, 3, 2).reshape(g * 512, n)


K, T, S, N, H = 512, 2048, 512, 512, 512


def setup_inputs():
    n = np.random.standard_normal
    s = mx_kscale(K)[:, None]
    u = mx_kscale(H)
    packed_xT = pack_weight(n((K, T)) * s)
    return {
        "x_words": packed_xT[0],
        "x_scales": packed_xT[1],
        "w1": (n((K, H)) / np.sqrt(K) / s).astype(np.float32),
        "w2": (n((K, H)) / np.sqrt(K) / s).astype(np.float32),
        "w3": (n((K, H)) / np.sqrt(K) / s).astype(np.float32),
        "gn": (np.random.uniform(0.5, 1.5, (H, 1)) * u[:, None]).astype(np.float32),
        "w4": (n((H, N)) / np.sqrt(H) / u[:, None]).astype(np.float32),
        "offs": striped(np.random.permutation(T)[:S]),
        "two": striped(np.random.permutation(T)[:S]),
        "three": striped(np.random.permutation(T)[:S]),
        "n1": striped8(np.stack([np.random.permutation(S) for _ in range(8)])),
        "n2": striped8(np.stack([np.random.permutation(S) for _ in range(8)])),
        "n3": striped8(np.stack([np.random.permutation(S) for _ in range(8)])),
        "n4": striped8(np.stack([np.random.permutation(S) for _ in range(8)])),
        "n5": striped8(np.stack([np.random.permutation(S) for _ in range(8)])),
        "n6": striped8(np.stack([np.random.permutation(S) for _ in range(8)])),
    }


def reference(x_words, x_scales, w1, w2, w3, gn, w4, offs, two, three, n1, n2, n3, n4, n5, n6):
    xq = unpack_weight(x_words, x_scales)[:, unstriped(offs)]
    y = mxq(f64(w1), 0, "e4m3").T @ xq
    x_two = unpack_weight(x_words, x_scales)[:, unstriped(two)]
    d = mxq(f64(w2), 0, "e4m3").T @ x_two
    m1 = y[np.arange(H)[:, None], runs(n1, H)] - (np.tanh(d) * (d[np.arange(H)[:, None], runs(n2, H)]))
    x_three = unpack_weight(x_words, x_scales)[:, unstriped(three)]
    b = mxq(f64(w3), 0, "e4m3").T @ x_three
    z = f64(gn) * (np.maximum(m1, b[np.arange(H)[:, None], runs(n4, H)]) - (np.minimum(m1[np.arange(H)[:, None], runs(n3, H)], b)))
    h = mxq(f64(w4), 0, "e4m3").T @ mxq(z, 0, "e4m3")
    st = h + h[np.arange(N)[:, None], runs(n5, N)]
    return st * (np.tanh(st[np.arange(N)[:, None], runs(n6, N)]))

@@ -1,0 +1,165 @@
+from contextlib import ExitStack
+
+import concourse.mybir as mybir
+
+F32 = mybir.dt.float32
+BF16 = mybir.dt.bfloat16
+I32 = mybir.dt.int32
+U32 = mybir.dt.uint32
+U16 = mybir.dt.uint16
+U8 = mybir.dt.uint8
+FP8X4 = mybir.dt.float8_e4m3fn_x4
+ALU = mybir.AluOpType
+ACT = mybir.ActivationFunctionType
+
+P = 128
+K, T, S, N, H = 512, 2048, 512, 512, 512
+NT = 4
+CH = 256
+FLOPS = 4 * 2 * 512 * 512 * 512
+
+
+def tile_picked_triosoftbmaxbhopp_none_p_kernel(tc, x_words, x_scales, w1, w2, w3, gn, w4, offs, two, three, n1, n2, n3, n4, n5, n6, out):
+    nc = tc.nc
+    with ExitStack() as ctx:
+        lists = ctx.enter_context(tc.tile_pool(name="lists", bufs=1))
+        keep = ctx.enter_context(tc.tile_pool(name="keep", bufs=1))
+        psum = ctx.enter_context(tc.psum_pool(name="psum", bufs=1))
+
+        def load_list(src, name):
+            t = lists.tile([P, S // 16], U16, name=name)
+            nc.sync.dma_start(t[:], src)
+            return t
+
+        def sb(shape, dtype, name):
+            return keep.tile(shape, dtype, name=name, align_bytes=64)
+
+        x_sc = sb([P, T], U8, "x_sc")
+        nc.gpsimd.memset(x_sc[:].bitcast(I32), 0)
+        l_two = load_list(two, "l_two")
+        for q in range(4):
+            nc.scalar.dma_start(x_sc[32 * q : 32 * q + 4, :].bitcast(I32), x_scales[0, 4 * q : 4 * q + 4, :].bitcast(I32))
+        l_offs = load_list(offs, "l_offs")
+        l_three = load_list(three, "l_three")
+        l_n2 = load_list(n2, "l_n2")
+
+        def load_weight(w, name):
+            raw = sb([P, 4, H], F32, name)
+            nc.sync.dma_start(raw[:], w.rearrange("(p j) c -> p j c", j=4))
+            return raw
+
+        raw2 = load_weight(w2, "raw2")
+        x_w = sb([P, T], U32, "x_w")
+        nc.sync.dma_start(x_w[:].bitcast(I32), x_words[0].rearrange("p n t -> p (n t)").bitcast(I32))
+        raw1 = load_weight(w1, "raw1")
+        l_n1 = load_list(n1, "l_n1")
+        l_n3 = load_list(n3, "l_n3")
+        raw3 = load_weight(w3, "raw3")
+        l_n4 = load_list(n4, "l_n4")
+        gain = [sb([P, 1], F32, "gain%d" % t) for t in range(NT)]
+        gn_rows = gn.rearrange("(b t e) o -> t b e o", t=NT, e=8)
+        raw4 = sb([P, 4, N], F32, "raw4")
+        w4_rows = w4.rearrange("(b t e) c -> t b e c", t=NT, e=8)
+        with nc.allow_non_contiguous_dma(reason="one gain a partition"):
+            for t in range(NT):
+                nc.sync.dma_start(gain[t][:], gn_rows[t])
+        for t in range(NT):
+            nc.sync.dma_start(raw4[:, t, :], w4_rows[t])
+        l_n5 = load_list(n5, "l_n5")
+        l_n6 = load_list(n6, "l_n6")
+
+        warm = sb([P, 2], F32, "warm")
+        nc.gpsimd.memset(warm[:, 0:1], 0.0)
+        nc.scalar.activation(warm[:, 1:2], warm[:, 0:1], ACT.Sigmoid)
+
+        dwin = [sb([P, 2 * S], F32, "dwin%d" % t) for t in range(NT)]
+        for t in range(NT):
+            nc.gpsimd.memset(dwin[t][:, S:], 0.0)
+
+        def pick_scales(lst, name):
+            g = sb([P, S], U8, name)
+            nc.vector.tensor_copy(g[:], x_sc[:].indirect(lst[:]))
+            return g
+
+        def pick_words(lst, name):
+            g = sb([P, S], U32, name)
+            nc.vector.tensor_copy(g[:], x_w[:].indirect(lst[:]))
+            return g
+
+        def quantise_weight(raw, t, name):
+            grp = sb([P, P, 4], BF16, "grp_%s%d" % (name, t))
+            nc.scalar.copy(
+                grp[:].rearrange("p (b h i) j -> p b h j i", h=2, i=4),
+                raw[:].rearrange("p j (b t h i) -> p t b h j i", t=NT, h=2, i=4)[:, t],
+            )
+            codes = sb([P, P], U32, "codes_%s%d" % (name, t))
+            scales = sb([P, P], U8, "scales_%s%d" % (name, t))
+            nc.vector.quantize_mx(out=codes[:].bitcast(FP8X4), scales=scales[:], in_=grp[:].rearrange("p c j -> p (c j)"))
+            return codes, scales
+
+        def product(acc, wq, words, scales):
+            nc.tensor.matmul_mx(out=acc, lhsT=wq[0][:].bitcast(FP8X4), lhsT_scale=wq[1][:], rhs=words.bitcast(FP8X4), rhs_scale=scales, start=True, stop=True)
+
+        s_two = pick_scales(l_two, "s_two")
+        s_offs = pick_scales(l_offs, "s_offs")
+        s_three = pick_scales(l_three, "s_three")
+        q2 = [quantise_weight(raw2, t, "w2") for t in range(NT)]
+        g_two = pick_words(l_two, "g_two")
+        g_offs = pick_words(l_offs, "g_offs")
+        g_three = pick_words(l_three, "g_three")
+
+        ywin = [sb([P, 2 * S], F32, "ywin%d" % t) for t in range(NT)]
+        mwin = [sb([P, 2 * S], F32, "mwin%d" % t) for t in range(NT)]
+        bwin = [sb([P, S], F32, "bwin%d" % t) for t in range(NT)]
+        low = [sb([P, S], F32, "low%d" % t) for t in range(NT)]
+        lowg = [sb([P, S], F32, "lowg%d" % t) for t in range(NT)]
+        for t in range(NT):
+            acc = psum.tile([P, S], F32, name="mm", bufs=4)
+            product(acc[:], q2[t], g_two[:], s_two[:])
+            nc.scalar.activation(ywin[t][:, S:], acc[:], ACT.Tanh)
+            nc.scalar.copy(dwin[t][:, :S], acc[:])
+            q1 = quantise_weight(raw1, t, "w1")
+            acc = psum.tile([P, S], F32, name="mm", bufs=4)
+            product(acc[:], q1, g_offs[:], s_offs[:])
+            nc.scalar.copy(ywin[t][:, :S], acc[:])
+            nc.vector.tensor_tensor(mwin[t][:, S:], dwin[t][:].indirect(l_n2[:]), ywin[t][:, S:], ALU.mult)
+            nc.vector.tensor_tensor(mwin[t][:, :S], ywin[t][:].indirect(l_n1[:]), mwin[t][:, S:], ALU.subtract)
+            q3 = quantise_weight(raw3, t, "w3")
+            acc = psum.tile([P, S], F32, name="mm", bufs=4)
+            product(acc[:], q3, g_three[:], s_three[:])
+            nc.scalar.copy(bwin[t][:], acc[:])
+            m3 = keep.tile([P, S], F32, name="m3", bufs=2, align_bytes=64)
+            nc.vector.tensor_copy(m3[:], mwin[t][:].indirect(l_n3[:]))
+            nc.vector.tensor_tensor(low[t][:], m3[:], bwin[t][:], ALU.min)
+            nc.scalar.activation(lowg[t][:], low[t][:], ACT.Copy, scale=gain[t][:])
+        q4 = [quantise_weight(raw4, t, "w4") for t in range(NT)]
+
+        swin = [sb([P, 2 * S], F32, "swin%d" % t) for t in range(NT)]
+        hacc = [psum.tile([P, S], F32, name="h%d" % t) for t in range(NT)]
+        for c in range(S // CH):
+            cols = slice(c * CH, (c + 1) * CH)
+            zb = sb([P, NT, CH], BF16, "zb%d" % c)
+            for t in range(NT):
+                b4 = keep.tile([P, CH], F32, name="b4", bufs=3, align_bytes=64)
+                nc.vector.tensor_copy(b4[:], bwin[t][:].indirect(l_n4[:, c * CH // 16 : (c + 1) * CH // 16]))
+                high = keep.tile([P, CH], F32, name="high", bufs=3, align_bytes=64)
+                nc.vector.tensor_tensor(high[:], b4[:], mwin[t][:, cols], ALU.max)
+                nc.vector.scalar_tensor_tensor(zb[:, t, :], high[:], gain[t][:], lowg[t][:, cols], ALU.mult, ALU.subtract)
+            zg = sb([P, CH, 4], BF16, "zg%d" % c)
+            nc.scalar.copy(zg[:].rearrange("p (c i) t -> p c t i", i=4), zb[:].rearrange("p t (c i) -> p c t i", i=4))
+            zq = sb([P, CH], U32, "zq%d" % c)
+            zs = sb([P, CH], U8, "zs%d" % c)
+            nc.vector.quantize_mx(out=zq[:].bitcast(FP8X4), scales=zs[:], in_=zg[:].rearrange("p c t -> p (c t)"))
+            for t in range(NT):
+                product(hacc[t][:, cols], q4[t], zq[:], zs[:])
+                nc.scalar.activation(dwin[t][:, cols], hacc[t][:, cols], ACT.Copy, scale=2.0)
+                nc.scalar.activation(swin[t][:, S + c * CH : S + (c + 1) * CH], hacc[t][:, cols], ACT.Copy, scale=2.0)
+
+        out_rows = out.rearrange("(b t e) c -> t b e c", t=NT, e=8)
+        for t in range(NT):
+            nc.vector.tensor_tensor(swin[t][:, :S], dwin[t][:].indirect(l_n5[:]), swin[t][:, S:], ALU.add)
+            sig = sb([P, S], F32, "sig%d" % t)
+            nc.scalar.activation(sig[:], swin[t][:].indirect(l_n6[:]), ACT.Sigmoid)
+            res = sb([P, S], F32, "res%d" % t)
+            nc.vector.scalar_tensor_tensor(res[:], sig[:], 0.5, swin[t][:, :S], ALU.subtract, ALU.mult)
+            nc.sync.dma_start(out_rows[t], res[:])

@@ -1,6 +1,7 @@
 from contextlib import ExitStack
 
 import concourse.mybir as mybir
+from concourse.masks import make_identity
 
 F32 = mybir.dt.float32
 BF16 = mybir.dt.bfloat16
@@ -15,7 +16,7 @@ ACT = mybir.ActivationFunctionType
 P = 128
 K, T, S, N, H = 512, 2048, 512, 512, 512
 NT = 4
-CH = 256
+NB = 4
 FLOPS = 4 * 2 * 512 * 512 * 512
 
 
@@ -36,33 +37,30 @@ def tile_picked_triosoftbmaxbhopp_none_p_kernel(tc, x_words, x_scales, w1, w2, w
 
         x_sc = sb([P, T], U8, "x_sc")
         nc.gpsimd.memset(x_sc[:].bitcast(I32), 0)
-        l_two = load_list(two, "l_two")
-        for q in range(4):
-            nc.scalar.dma_start(x_sc[32 * q : 32 * q + 4, :].bitcast(I32), x_scales[0, 4 * q : 4 * q + 4, :].bitcast(I32))
-        l_offs = load_list(offs, "l_offs")
-        l_three = load_list(three, "l_three")
-        l_n2 = load_list(n2, "l_n2")
 
         def load_weight(w, name):
             raw = sb([P, 4, H], F32, name)
             nc.sync.dma_start(raw[:], w.rearrange("(p j) c -> p j c", j=4))
             return raw
 
-        raw2 = load_weight(w2, "raw2")
+        l_two = load_list(two, "l_two")
+        l_offs = load_list(offs, "l_offs")
+        l_three = load_list(three, "l_three")
         x_w = sb([P, T], U32, "x_w")
         nc.sync.dma_start(x_w[:].bitcast(I32), x_words[0].rearrange("p n t -> p (n t)").bitcast(I32))
-        raw1 = load_weight(w1, "raw1")
+        raw2 = load_weight(w2, "raw2")
+        l_n2 = load_list(n2, "l_n2")
         l_n1 = load_list(n1, "l_n1")
-        l_n3 = load_list(n3, "l_n3")
+        for q in range(4):
+            nc.sync.dma_start(x_sc[32 * q : 32 * q + 4, :].bitcast(I32), x_scales[0, 4 * q : 4 * q + 4, :].bitcast(I32))
+        raw1 = load_weight(w1, "raw1")
         raw3 = load_weight(w3, "raw3")
+        l_n3 = load_list(n3, "l_n3")
         l_n4 = load_list(n4, "l_n4")
-        gain = [sb([P, 1], F32, "gain%d" % t) for t in range(NT)]
-        gn_rows = gn.rearrange("(b t e) o -> t b e o", t=NT, e=8)
+        gain = sb([P, 4], F32, "gain")
+        nc.sync.dma_start(gain[:], gn.rearrange("(p s) o -> p (s o)", s=4))
         raw4 = sb([P, 4, N], F32, "raw4")
         w4_rows = w4.rearrange("(b t e) c -> t b e c", t=NT, e=8)
-        with nc.allow_non_contiguous_dma(reason="one gain a partition"):
-            for t in range(NT):
-                nc.sync.dma_start(gain[t][:], gn_rows[t])
         for t in range(NT):
             nc.sync.dma_start(raw4[:, t, :], w4_rows[t])
         l_n5 = load_list(n5, "l_n5")
@@ -72,94 +70,197 @@ def tile_picked_triosoftbmaxbhopp_none_p_kernel(tc, x_words, x_scales, w1, w2, w
         nc.gpsimd.memset(warm[:, 0:1], 0.0)
         nc.scalar.activation(warm[:, 1:2], warm[:, 0:1], ACT.Sigmoid)
 
+        ident = sb([P, P], F32, "ident")
+        make_identity(nc, ident[:])
         dwin = [sb([P, 2 * S], F32, "dwin%d" % t) for t in range(NT)]
         for t in range(NT):
             nc.gpsimd.memset(dwin[t][:, S:], 0.0)
 
-        def pick_scales(lst, name):
-            g = sb([P, S], U8, name)
+        def pick_scales(lst, name, tag):
+            g = keep.tile([P, S], U8, name=name, tag=tag, align_bytes=64)
             nc.vector.tensor_copy(g[:], x_sc[:].indirect(lst[:]))
             return g
 
-        def pick_words(lst, name):
-            g = sb([P, S], U32, name)
+        def pick_words(lst, name, tag):
+            g = keep.tile([P, S], U32, name=name, tag=tag, align_bytes=64)
             nc.vector.tensor_copy(g[:], x_w[:].indirect(lst[:]))
             return g
 
-        def quantise_weight(raw, t, name):
-            grp = sb([P, P, 4], BF16, "grp_%s%d" % (name, t))
-            nc.scalar.copy(
-                grp[:].rearrange("p (b h i) j -> p b h j i", h=2, i=4),
-                raw[:].rearrange("p j (b t h i) -> p t b h j i", t=NT, h=2, i=4)[:, t],
-            )
-            codes = sb([P, P], U32, "codes_%s%d" % (name, t))
-            scales = sb([P, P], U8, "scales_%s%d" % (name, t))
-            nc.vector.quantize_mx(out=codes[:].bitcast(FP8X4), scales=scales[:], in_=grp[:].rearrange("p c j -> p (c j)"))
-            return codes, scales
+        def quantise_weight(raw, name, tiles):
+            grp = keep.tile([P, len(tiles), P, 4], BF16, name="grp", tag="grp_%s%d" % (name, tiles[0]), align_bytes=64)
+            for i, t in enumerate(tiles):
+                nc.scalar.copy(
+                    grp[:, i].rearrange("p (b h i) j -> p b h j i", h=2, i=4),
+                    raw[:].rearrange("p j (b t h i) -> p t b h j i", t=NT, h=2, i=4)[:, t],
+                )
+            codes = sb([P, len(tiles) * P], U32, "codes_%s%d" % (name, tiles[0]))
+            scales = sb([P, len(tiles) * P], U8, "scales_%s%d" % (name, tiles[0]))
+            nc.vector.quantize_mx(out=codes[:].bitcast(FP8X4), scales=scales[:], in_=grp[:].rearrange("p t c j -> p (t c j)"))
+            return [(codes[:, i * P : (i + 1) * P], scales[:, i * P : (i + 1) * P]) for i in range(len(tiles))]
 
         def product(acc, wq, words, scales):
-            nc.tensor.matmul_mx(out=acc, lhsT=wq[0][:].bitcast(FP8X4), lhsT_scale=wq[1][:], rhs=words.bitcast(FP8X4), rhs_scale=scales, start=True, stop=True)
+            nc.tensor.matmul_mx(out=acc, lhsT=wq[0].bitcast(FP8X4), lhsT_scale=wq[1], rhs=words.bitcast(FP8X4), rhs_scale=scales, start=True, stop=True)
 
-        s_two = pick_scales(l_two, "s_two")
-        s_offs = pick_scales(l_offs, "s_offs")
-        s_three = pick_scales(l_three, "s_three")
-        q2 = [quantise_weight(raw2, t, "w2") for t in range(NT)]
-        g_two = pick_words(l_two, "g_two")
-        g_offs = pick_words(l_offs, "g_offs")
-        g_three = pick_words(l_three, "g_three")
+        def bank(group, i):
+            return psum.tile([P, S], F32, name="%s%d" % (group, i))
+
+        g_two = pick_words(l_two, "g_two", "g_two")
+        g_offs = pick_words(l_offs, "g_offs", "g_offs")
+        s_two = pick_scales(l_two, "s_two", "s_two")
+        q2 = quantise_weight(raw2, "w2", (0, 1)) + quantise_weight(raw2, "w2", (2, 3))
+        g_three = pick_words(l_three, "g_three", "grp_w20")
+        s_offs = pick_scales(l_offs, "s_offs", "grp_w22")
 
         ywin = [sb([P, 2 * S], F32, "ywin%d" % t) for t in range(NT)]
         mwin = [sb([P, 2 * S], F32, "mwin%d" % t) for t in range(NT)]
-        bwin = [sb([P, S], F32, "bwin%d" % t) for t in range(NT)]
-        low = [sb([P, S], F32, "low%d" % t) for t in range(NT)]
-        lowg = [sb([P, S], F32, "lowg%d" % t) for t in range(NT)]
+        nb = [sb([P, S], F32, "nb%d" % t) for t in range(NT)]
+
+        dacc = [bank("a", t) for t in range(NT)]
+        yacc = [bank("z", t) for t in range(NT)]
         for t in range(NT):
-            acc = psum.tile([P, S], F32, name="mm", bufs=4)
-            product(acc[:], q2[t], g_two[:], s_two[:])
-            nc.scalar.activation(ywin[t][:, S:], acc[:], ACT.Tanh)
-            nc.scalar.copy(dwin[t][:, :S], acc[:])
-            q1 = quantise_weight(raw1, t, "w1")
-            acc = psum.tile([P, S], F32, name="mm", bufs=4)
-            product(acc[:], q1, g_offs[:], s_offs[:])
-            nc.scalar.copy(ywin[t][:, :S], acc[:])
+            product(dacc[t][:], q2[t], g_two[:], s_two[:])
+
+        def d_side(t):
+            nc.scalar.activation(ywin[t][:, S:], dacc[t][:], ACT.Tanh)
+            nc.scalar.copy(dwin[t][:, :S], dacc[t][:])
             nc.vector.tensor_tensor(mwin[t][:, S:], dwin[t][:].indirect(l_n2[:]), ywin[t][:, S:], ALU.mult)
+
+        def y_side(t):
+            product(yacc[t][:], q1[t], g_offs[:], s_offs[:])
+            nc.scalar.copy(ywin[t][:, :S], yacc[t][:])
             nc.vector.tensor_tensor(mwin[t][:, :S], ywin[t][:].indirect(l_n1[:]), mwin[t][:, S:], ALU.subtract)
-            q3 = quantise_weight(raw3, t, "w3")
-            acc = psum.tile([P, S], F32, name="mm", bufs=4)
-            product(acc[:], q3, g_three[:], s_three[:])
-            nc.scalar.copy(bwin[t][:], acc[:])
-            m3 = keep.tile([P, S], F32, name="m3", bufs=2, align_bytes=64)
-            nc.vector.tensor_copy(m3[:], mwin[t][:].indirect(l_n3[:]))
-            nc.vector.tensor_tensor(low[t][:], m3[:], bwin[t][:], ALU.min)
-            nc.scalar.activation(lowg[t][:], low[t][:], ACT.Copy, scale=gain[t][:])
-        q4 = [quantise_weight(raw4, t, "w4") for t in range(NT)]
+
+        q1 = quantise_weight(raw1, "w1", (0, 1))
+        s_three = pick_scales(l_three, "s_three", "grp_w10")
+        d_side(0)
+        d_side(1)
+        y_side(0)
+        y_side(1)
+        q1 = q1 + quantise_weight(raw1, "w1", (2, 3))
+        gps = bank("a", 0)
+        for j in range(4):
+            nc.tensor.transpose(gps[:, j * P : (j + 1) * P], gain[:, j : j + 1].to_broadcast([P, P]), ident[:])
+        gain_row = sb([P, 2, 256], F32, "gain_row")
+        for u in range(2):
+            nc.scalar.copy(
+                gain_row[:, u, :].rearrange("p (b x j e) -> p b x j e", x=2, j=4, e=2),
+                gps[:].rearrange("p (j b u e x) -> p u b x j e", j=4, u=2, e=2, x=2)[:, u],
+            )
+
+        d_side(2)
+        d_side(3)
+        q3 = quantise_weight(raw3, "w3", (0, 1, 2, 3))
+        y_side(2)
+        y_side(3)
+        for t in range(NT):
+            acc = bank("a", t)
+            product(acc[:], q3[t], g_three[:], s_three[:])
+            nc.scalar.activation(nb[t][:], acc[:], ACT.Copy, scale=-1.0)
+
+        zt = [bank("z", c) for c in range(NB)]
+
+        def add_turned(src, c, t, start=False, stop=False):
+            nc.tensor.matmul(zt[c][:, t * P : (t + 1) * P], lhsT=src, rhs=ident[:], is_transpose=True, start=start, stop=stop)
+
+        for t in range(NT):
+            for c in range(NB):
+                cols = slice(c * P, (c + 1) * P)
+                add_turned(mwin[t][:, cols], c, t, start=(t == 0))
+                add_turned(nb[t][:, cols], c, t)
+
+        q4 = quantise_weight(raw4, "w4", (0, 1, 2, 3))
+
+        def slot(shape, dtype, name, tag):
+            return keep.tile(shape, dtype, name=name, tag=tag, align_bytes=64)
+
+        def low_side(half, t, gap):
+            c0 = half * 2 * P
+            nc.vector.tensor_tensor(gap, mwin[t][:].indirect(l_n3[:, c0 // 16 : (c0 + 2 * P) // 16]), nb[t][:, c0 : c0 + 2 * P], ALU.add)
+            nc.scalar.activation(gap, gap, ACT.Relu, scale=-1.0)
+            for i in range(2):
+                add_turned(gap[:, i * P : (i + 1) * P], 2 * half + i, t)
+
+        def high_side(c, gap, split):
+            for t in range(NT):
+                part = gap[:, t * P : (t + 1) * P]
+                nc.vector.tensor_tensor(part, nb[t][:].indirect(l_n4[:, c * P // 16 : (c + 1) * P // 16]), mwin[t][:, c * P : (c + 1) * P], ALU.add)
+                if split:
+                    nc.scalar.activation(part, part, ACT.Relu, scale=-1.0)
+            if not split:
+                nc.scalar.activation(gap, gap, ACT.Relu, scale=-1.0)
+            for t in range(NT):
+                add_turned(gap[:, t * P : (t + 1) * P], c, t, stop=(t == NT - 1))
+
+        zg = [slot([P, 2 * P, 4], BF16, "zg", "zg%d" % half) for half in range(2)]
+
+        def turn_back(c):
+            zrow = slot([P, 2, P, 2], BF16, "zrow", "zrow%d" % c)
+            nc.vector.tensor_tensor(
+                zrow[:],
+                zt[c][:].rearrange("p (u e f) -> p u f e", u=2, e=2),
+                gain_row[:].rearrange("p u (f e) -> p u f e", e=2),
+                ALU.mult,
+            )
+            pairs = zrow[:].rearrange("p u f e -> p (u f e)").bitcast(F32)
+            back = bank("z", c)
+            for u in range(2):
+                nc.tensor.transpose(back[:, u * P : (u + 1) * P], pairs[:, u * P : (u + 1) * P], ident[:])
+            nc.scalar.copy(
+                zg[c // 2][:, c % 2 * P : (c % 2 + 1) * P, :].rearrange("p c t -> p (c t)").bitcast(F32).rearrange("p (c u) -> p c u", u=2),
+                back[:, : 2 * P].rearrange("p (u c) -> p c u", u=2),
+            )
 
         swin = [sb([P, 2 * S], F32, "swin%d" % t) for t in range(NT)]
-        hacc = [psum.tile([P, S], F32, name="h%d" % t) for t in range(NT)]
-        for c in range(S // CH):
-            cols = slice(c * CH, (c + 1) * CH)
-            zb = sb([P, NT, CH], BF16, "zb%d" % c)
-            for t in range(NT):
-                b4 = keep.tile([P, CH], F32, name="b4", bufs=3, align_bytes=64)
-                nc.vector.tensor_copy(b4[:], bwin[t][:].indirect(l_n4[:, c * CH // 16 : (c + 1) * CH // 16]))
-                high = keep.tile([P, CH], F32, name="high", bufs=3, align_bytes=64)
-                nc.vector.tensor_tensor(high[:], b4[:], mwin[t][:, cols], ALU.max)
-                nc.vector.scalar_tensor_tensor(zb[:, t, :], high[:], gain[t][:], lowg[t][:, cols], ALU.mult, ALU.subtract)
-            zg = sb([P, CH, 4], BF16, "zg%d" % c)
-            nc.scalar.copy(zg[:].rearrange("p (c i) t -> p c t i", i=4), zb[:].rearrange("p t (c i) -> p c t i", i=4))
-            zq = sb([P, CH], U32, "zq%d" % c)
-            zs = sb([P, CH], U8, "zs%d" % c)
-            nc.vector.quantize_mx(out=zq[:].bitcast(FP8X4), scales=zs[:], in_=zg[:].rearrange("p c t -> p (c t)"))
+        hacc = [bank("a", t) for t in range(NT)]
+
+        def last_product(c0, width):
+            cols = slice(c0, c0 + width)
+            zq = sb([P, width], U32, "zq%d" % c0)
+            zs = sb([P, width], U8, "zs%d" % c0)
+            src = zg[c0 // (2 * P)][:, c0 % (2 * P) : c0 % (2 * P) + width, :]
+            nc.vector.quantize_mx(out=zq[:].bitcast(FP8X4), scales=zs[:], in_=src.rearrange("p c t -> p (c t)"))
             for t in range(NT):
                 product(hacc[t][:, cols], q4[t], zq[:], zs[:])
-                nc.scalar.activation(dwin[t][:, cols], hacc[t][:, cols], ACT.Copy, scale=2.0)
-                nc.scalar.activation(swin[t][:, S + c * CH : S + (c + 1) * CH], hacc[t][:, cols], ACT.Copy, scale=2.0)
+
+        def leave_bank(t, c0, width, by_dma):
+            cols = slice(c0, c0 + width)
+            nc.scalar.activation(dwin[t][:, cols], hacc[t][:, cols], ACT.Copy, scale=2.0)
+            if by_dma:
+                nc.sync.dma_start(swin[t][:, S + c0 : S + c0 + width], dwin[t][:, cols])
+            else:
+                nc.scalar.activation(swin[t][:, S + c0 : S + c0 + width], hacc[t][:, cols], ACT.Copy, scale=2.0)
+
+        first = slot([P, NT * 2 * P], F32, "gaps_first", "gaps_first")
+        for t in range(NT):
+            low_side(0, t, first[:, t * 2 * P : (t + 1) * 2 * P])
+        high_side(0, slot([P, S], F32, "gap_high0", "high0")[:], False)
+        high_side(1, slot([P, S], F32, "gap_high1", "high1")[:], False)
+        turn_back(0)
+        turn_back(1)
+        mid = slot([P, S], F32, "gaps_mid", "high1")
+        low_side(1, 0, mid[:, : 2 * P])
+        low_side(1, 1, mid[:, 2 * P :])
+        last_product(0, 2 * P)
+        late = slot([P, 3 * S], F32, "gaps_late", "zg0")
+        low_side(1, 2, late[:, : 2 * P])
+        low_side(1, 3, late[:, 2 * P : S])
+        for t in range(NT):
+            leave_bank(t, 0, 2 * P, True)
+        high_side(2, late[:, S : 2 * S], False)
+        high_side(3, late[:, 2 * S :], True)
+        turn_back(2)
+        turn_back(3)
+        last_product(2 * P, 2 * P)
+        for t in range(NT):
+            leave_bank(t, 2 * P, 2 * P, False)
 
         out_rows = out.rearrange("(b t e) c -> t b e c", t=NT, e=8)
+        sig = [sb([P, S], F32, "sig%d" % t) for t in range(NT)]
+        pieces = [(t, 0, S) for t in range(NT - 1)] + [(NT - 1, 0, S // 2), (NT - 1, S // 2, S)]
         for t in range(NT):
             nc.vector.tensor_tensor(swin[t][:, :S], dwin[t][:].indirect(l_n5[:]), swin[t][:, S:], ALU.add)
-            sig = sb([P, S], F32, "sig%d" % t)
-            nc.scalar.activation(sig[:], swin[t][:].indirect(l_n6[:]), ACT.Sigmoid)
-            res = sb([P, S], F32, "res%d" % t)
-            nc.vector.scalar_tensor_tensor(res[:], sig[:], 0.5, swin[t][:, :S], ALU.subtract, ALU.mult)
-            nc.sync.dma_start(out_rows[t], res[:])
+        for t, lo, hi in pieces:
+            nc.scalar.activation(sig[t][:, lo:hi], swin[t][:].indirect(l_n6[:, lo // 16 : hi // 16]), ACT.Sigmoid)
+            res = sb([P, hi - lo], F32, "res%d_%d" % (t, lo))
+            nc.vector.scalar_tensor_tensor(res[:], sig[t][:, lo:hi], 0.5, swin[t][:, lo:hi], ALU.subtract, ALU.mult)
+            nc.sync.dma_start(out_rows[t][:, :, lo:hi], res[:])

@@ -46,24 +46,24 @@ def tile_picked_triosoftbmaxbhopp_none_p_kernel(tc, x_words, x_scales, w1, w2, w
         l_two = load_list(two, "l_two")
         l_offs = load_list(offs, "l_offs")
         l_three = load_list(three, "l_three")
-        x_w = sb([P, T], U32, "x_w")
-        nc.sync.dma_start(x_w[:].bitcast(I32), x_words[0].rearrange("p n t -> p (n t)").bitcast(I32))
-        raw2 = load_weight(w2, "raw2")
         l_n2 = load_list(n2, "l_n2")
         l_n1 = load_list(n1, "l_n1")
+        l_n3 = load_list(n3, "l_n3")
+        x_w = sb([P, T], U32, "x_w")
+        nc.sync.dma_start(x_w[:].bitcast(I32), x_words[0].rearrange("p n t -> p (n t)").bitcast(I32))
         for q in range(4):
             nc.sync.dma_start(x_sc[32 * q : 32 * q + 4, :].bitcast(I32), x_scales[0, 4 * q : 4 * q + 4, :].bitcast(I32))
-        raw1 = load_weight(w1, "raw1")
-        raw3 = load_weight(w3, "raw3")
-        l_n3 = load_list(n3, "l_n3")
         l_n4 = load_list(n4, "l_n4")
+        l_n5 = load_list(n5, "l_n5")
+        raw2 = load_weight(w2, "raw2")
+        raw1 = load_weight(w1, "raw1")
         gain = sb([P, 4], F32, "gain")
         nc.sync.dma_start(gain[:], gn.rearrange("(p s) o -> p (s o)", s=4))
+        raw3 = load_weight(w3, "raw3")
         raw4 = sb([P, 4, N], F32, "raw4")
         w4_rows = w4.rearrange("(b t e) c -> t b e c", t=NT, e=8)
         for t in range(NT):
             nc.sync.dma_start(raw4[:, t, :], w4_rows[t])
-        l_n5 = load_list(n5, "l_n5")
         l_n6 = load_list(n6, "l_n6")
 
         warm = sb([P, 2], F32, "warm")
@@ -86,17 +86,25 @@ def tile_picked_triosoftbmaxbhopp_none_p_kernel(tc, x_words, x_scales, w1, w2, w
             nc.vector.tensor_copy(g[:], x_w[:].indirect(lst[:]))
             return g
 
-        def quantise_weight(raw, name, tiles):
-            grp = keep.tile([P, len(tiles), P, 4], BF16, name="grp", tag="grp_%s%d" % (name, tiles[0]), align_bytes=64)
-            for i, t in enumerate(tiles):
-                nc.scalar.copy(
-                    grp[:, i].rearrange("p (b h i) j -> p b h j i", h=2, i=4),
-                    raw[:].rearrange("p j (b t h i) -> p t b h j i", t=NT, h=2, i=4)[:, t],
-                )
-            codes = sb([P, len(tiles) * P], U32, "codes_%s%d" % (name, tiles[0]))
-            scales = sb([P, len(tiles) * P], U8, "scales_%s%d" % (name, tiles[0]))
+        def weave_weight(raw, t, dst):
+            nc.scalar.copy(
+                dst.rearrange("p (b h i) j -> p b h j i", h=2, i=4),
+                raw[:].rearrange("p j (b t h i) -> p t b h j i", t=NT, h=2, i=4)[:, t],
+            )
+
+        def quantise_woven(grp, name):
+            count = grp.shape[1]
+            codes = sb([P, count * P], U32, "codes_" + name)
+            scales = sb([P, count * P], U8, "scales_" + name)
             nc.vector.quantize_mx(out=codes[:].bitcast(FP8X4), scales=scales[:], in_=grp[:].rearrange("p t c j -> p (t c j)"))
-            return [(codes[:, i * P : (i + 1) * P], scales[:, i * P : (i + 1) * P]) for i in range(len(tiles))]
+            return [(codes[:, i * P : (i + 1) * P], scales[:, i * P : (i + 1) * P]) for i in range(count)]
+
+        def quantise_weight(raw, name, tiles):
+            name = "%s%d" % (name, tiles[0])
+            grp = keep.tile([P, len(tiles), P, 4], BF16, name="grp", tag="grp_" + name, align_bytes=64)
+            for i, t in enumerate(tiles):
+                weave_weight(raw, t, grp[:, i])
+            return quantise_woven(grp, name)
 
         def product(acc, wq, words, scales):
             nc.tensor.matmul_mx(out=acc, lhsT=wq[0].bitcast(FP8X4), lhsT_scale=wq[1], rhs=words.bitcast(FP8X4), rhs_scale=scales, start=True, stop=True)
@@ -106,10 +114,11 @@ def tile_picked_triosoftbmaxbhopp_none_p_kernel(tc, x_words, x_scales, w1, w2, w
 
         g_two = pick_words(l_two, "g_two", "g_two")
         g_offs = pick_words(l_offs, "g_offs", "g_offs")
+        g_three = pick_words(l_three, "g_three", "g_three")
         s_two = pick_scales(l_two, "s_two", "s_two")
         q2 = quantise_weight(raw2, "w2", (0, 1)) + quantise_weight(raw2, "w2", (2, 3))
-        g_three = pick_words(l_three, "g_three", "grp_w20")
-        s_offs = pick_scales(l_offs, "s_offs", "grp_w22")
+        s_offs = pick_scales(l_offs, "s_offs", "grp_w20")
+        s_three = pick_scales(l_three, "s_three", "grp_w22")
 
         ywin = [sb([P, 2 * S], F32, "ywin%d" % t) for t in range(NT)]
         mwin = [sb([P, 2 * S], F32, "mwin%d" % t) for t in range(NT)]
@@ -130,13 +139,19 @@ def tile_picked_triosoftbmaxbhopp_none_p_kernel(tc, x_words, x_scales, w1, w2, w
             nc.scalar.copy(ywin[t][:, :S], yacc[t][:])
             nc.vector.tensor_tensor(mwin[t][:, :S], ywin[t][:].indirect(l_n1[:]), mwin[t][:, S:], ALU.subtract)
 
-        q1 = quantise_weight(raw1, "w1", (0, 1))
-        s_three = pick_scales(l_three, "s_three", "grp_w10")
+        q1 = quantise_weight(raw1, "w1", (0, 1, 2, 3))
         d_side(0)
-        d_side(1)
-        y_side(0)
-        y_side(1)
-        q1 = q1 + quantise_weight(raw1, "w1", (2, 3))
+        for t in range(1, NT):
+            if t == NT - 1:
+                q3 = quantise_weight(raw3, "w3", (0, 1, 2, 3))
+            d_side(t)
+            y_side(t - 1)
+        y_side(NT - 1)
+        for t in range(NT):
+            acc = bank("a", t)
+            product(acc[:], q3[t], g_three[:], s_three[:])
+            nc.scalar.activation(nb[t][:], acc[:], ACT.Copy, scale=-1.0)
+
         gps = bank("a", 0)
         for j in range(4):
             nc.tensor.transpose(gps[:, j * P : (j + 1) * P], gain[:, j : j + 1].to_broadcast([P, P]), ident[:])
@@ -147,15 +162,6 @@ def tile_picked_triosoftbmaxbhopp_none_p_kernel(tc, x_words, x_scales, w1, w2, w
                 gps[:].rearrange("p (j b u e x) -> p u b x j e", j=4, u=2, e=2, x=2)[:, u],
             )
 
-        d_side(2)
-        d_side(3)
-        q3 = quantise_weight(raw3, "w3", (0, 1, 2, 3))
-        y_side(2)
-        y_side(3)
-        for t in range(NT):
-            acc = bank("a", t)
-            product(acc[:], q3[t], g_three[:], s_three[:])
-            nc.scalar.activation(nb[t][:], acc[:], ACT.Copy, scale=-1.0)
 
         zt = [bank("z", c) for c in range(NB)]
 
@@ -164,11 +170,11 @@ def tile_picked_triosoftbmaxbhopp_none_p_kernel(tc, x_words, x_scales, w1, w2, w
 
         for t in range(NT):
             for c in range(NB):
-                cols = slice(c * P, (c + 1) * P)
-                add_turned(mwin[t][:, cols], c, t, start=(t == 0))
-                add_turned(nb[t][:, cols], c, t)
+                add_turned(mwin[t][:, c * P : (c + 1) * P], c, t, start=(t == 0))
+        for t in range(NT):
+            for c in range(NB):
+                add_turned(nb[t][:, c * P : (c + 1) * P], c, t)
 
-        q4 = quantise_weight(raw4, "w4", (0, 1, 2, 3))
 
         def slot(shape, dtype, name, tag):
             return keep.tile(shape, dtype, name=name, tag=tag, align_bytes=64)
@@ -180,16 +186,11 @@ def tile_picked_triosoftbmaxbhopp_none_p_kernel(tc, x_words, x_scales, w1, w2, w
             for i in range(2):
                 add_turned(gap[:, i * P : (i + 1) * P], 2 * half + i, t)
 
-        def high_side(c, gap, split):
-            for t in range(NT):
-                part = gap[:, t * P : (t + 1) * P]
-                nc.vector.tensor_tensor(part, nb[t][:].indirect(l_n4[:, c * P // 16 : (c + 1) * P // 16]), mwin[t][:, c * P : (c + 1) * P], ALU.add)
-                if split:
-                    nc.scalar.activation(part, part, ACT.Relu, scale=-1.0)
-            if not split:
-                nc.scalar.activation(gap, gap, ACT.Relu, scale=-1.0)
-            for t in range(NT):
-                add_turned(gap[:, t * P : (t + 1) * P], c, t, stop=(t == NT - 1))
+        def high_side(c0, width, t, gap):
+            nc.vector.tensor_tensor(gap, nb[t][:].indirect(l_n4[:, c0 // 16 : (c0 + width) // 16]), mwin[t][:, c0 : c0 + width], ALU.add)
+            nc.scalar.activation(gap, gap, ACT.Relu, scale=-1.0)
+            for i in range(width // P):
+                add_turned(gap[:, i * P : (i + 1) * P], c0 // P + i, t, stop=(t == NT - 1))
 
         zg = [slot([P, 2 * P, 4], BF16, "zg", "zg%d" % half) for half in range(2)]
 
@@ -213,46 +214,53 @@ def tile_picked_triosoftbmaxbhopp_none_p_kernel(tc, x_words, x_scales, w1, w2, w
         swin = [sb([P, 2 * S], F32, "swin%d" % t) for t in range(NT)]
         hacc = [bank("a", t) for t in range(NT)]
 
-        def last_product(c0, width):
-            cols = slice(c0, c0 + width)
+        def last_product(c0, width, accs):
             zq = sb([P, width], U32, "zq%d" % c0)
             zs = sb([P, width], U8, "zs%d" % c0)
             src = zg[c0 // (2 * P)][:, c0 % (2 * P) : c0 % (2 * P) + width, :]
             nc.vector.quantize_mx(out=zq[:].bitcast(FP8X4), scales=zs[:], in_=src.rearrange("p c t -> p (c t)"))
             for t in range(NT):
-                product(hacc[t][:, cols], q4[t], zq[:], zs[:])
+                product(accs[t], q4[t], zq[:], zs[:])
 
-        def leave_bank(t, c0, width, by_dma):
+        def leave_bank(t, c0, width, acc, by_dma):
             cols = slice(c0, c0 + width)
-            nc.scalar.activation(dwin[t][:, cols], hacc[t][:, cols], ACT.Copy, scale=2.0)
+            nc.scalar.activation(dwin[t][:, cols], acc, ACT.Copy, scale=2.0)
             if by_dma:
                 nc.sync.dma_start(swin[t][:, S + c0 : S + c0 + width], dwin[t][:, cols])
             else:
-                nc.scalar.activation(swin[t][:, S + c0 : S + c0 + width], hacc[t][:, cols], ACT.Copy, scale=2.0)
+                nc.scalar.activation(swin[t][:, S + c0 : S + c0 + width], acc, ACT.Copy, scale=2.0)
 
-        first = slot([P, NT * 2 * P], F32, "gaps_first", "gaps_first")
+        HALF = 2 * P
+        grp4 = sb([P, NT, P, 4], BF16, "grp_w4")
         for t in range(NT):
-            low_side(0, t, first[:, t * 2 * P : (t + 1) * 2 * P])
-        high_side(0, slot([P, S], F32, "gap_high0", "high0")[:], False)
-        high_side(1, slot([P, S], F32, "gap_high1", "high1")[:], False)
+            low_side(0, t, sb([P, HALF], F32, "low%d" % t)[:])
+            high_side(0, HALF, t, slot([P, HALF], F32, "high", "high%d" % t)[:])
+            weave_weight(raw4, t, grp4[:, t])
+        q4 = quantise_woven(grp4, "w4")
+        low_side(1, 0, sb([P, HALF], F32, "low4")[:])
         turn_back(0)
         turn_back(1)
-        mid = slot([P, S], F32, "gaps_mid", "high1")
-        low_side(1, 0, mid[:, : 2 * P])
-        low_side(1, 1, mid[:, 2 * P :])
-        last_product(0, 2 * P)
-        late = slot([P, 3 * S], F32, "gaps_late", "zg0")
-        low_side(1, 2, late[:, : 2 * P])
-        low_side(1, 3, late[:, 2 * P : S])
+        mid = slot([P, S], F32, "gaps_mid", "high%d" % (NT - 1))
+        low_side(1, 1, mid[:, :HALF])
+        low_side(1, 2, mid[:, HALF:])
+        last_product(0, HALF, [hacc[t][:, :HALF] for t in range(NT)])
+        late = slot([P, HALF + 2 * S], F32, "gaps_late", "zg0")
+        low_side(1, 3, late[:, :HALF])
         for t in range(NT):
-            leave_bank(t, 0, 2 * P, True)
-        high_side(2, late[:, S : 2 * S], False)
-        high_side(3, late[:, 2 * S :], True)
+            leave_bank(t, 0, HALF, hacc[t][:, :HALF], True)
+        for c in (2, 3):
+            for t in range(NT):
+                at = HALF + (c - 2) * S + t * P
+                high_side(c * P, P, t, late[:, at : at + P])
         turn_back(2)
         turn_back(3)
-        last_product(2 * P, 2 * P)
-        for t in range(NT):
-            leave_bank(t, 2 * P, 2 * P, False)
+        last_product(2 * P, P, [hacc[t][:, 2 * P : 3 * P] for t in range(NT)])
+        leave_bank(0, 2 * P, P, hacc[0][:, 2 * P : 3 * P], False)
+        tail = bank("z", 0)
+        last_product(3 * P, P, [tail[:, :P]] + [hacc[t][:, 3 * P :] for t in range(1, NT)])
+        leave_bank(0, 3 * P, P, tail[:, :P], False)
+        for t in range(1, NT):
+            leave_bank(t, HALF, HALF, hacc[t][:, HALF:], False)
 
         out_rows = out.rearrange("(b t e) c -> t b e c", t=NT, e=8)
         sig = [sb([P, S], F32, "sig%d" % t) for t in range(NT)]

@@ -74,7 +74,7 @@ def tile_picked_triosoftbmaxbhopp_none_p_kernel(tc, x_words, x_scales, w1, w2, w
         make_identity(nc, ident[:])
         dwin = [sb([P, 2 * S], F32, "dwin%d" % t) for t in range(NT)]
         for t in range(NT):
-            nc.gpsimd.memset(dwin[t][:, S:], 0.0)
+            nc.vector.memset(dwin[t][:, S:], 0.0)
 
         def pick_scales(lst, name, tag):
             g = keep.tile([P, S], U8, name=name, tag=tag, align_bytes=64)
@@ -92,9 +92,9 @@ def tile_picked_triosoftbmaxbhopp_none_p_kernel(tc, x_words, x_scales, w1, w2, w
                 raw[:].rearrange("p j (b t h i) -> p t b h j i", t=NT, h=2, i=4)[:, t],
             )
 
-        def quantise_woven(grp, name):
+        def quantise_woven(grp, name, tag):
             count = grp.shape[1]
-            codes = sb([P, count * P], U32, "codes_" + name)
+            codes = keep.tile([P, count * P], U32, name="codes_" + name, tag=tag, align_bytes=64)
             scales = sb([P, count * P], U8, "scales_" + name)
             nc.vector.quantize_mx(out=codes[:].bitcast(FP8X4), scales=scales[:], in_=grp[:].rearrange("p t c j -> p (t c j)"))
             return [(codes[:, i * P : (i + 1) * P], scales[:, i * P : (i + 1) * P]) for i in range(count)]
@@ -104,7 +104,7 @@ def tile_picked_triosoftbmaxbhopp_none_p_kernel(tc, x_words, x_scales, w1, w2, w
             grp = keep.tile([P, len(tiles), P, 4], BF16, name="grp", tag="grp_" + name, align_bytes=64)
             for i, t in enumerate(tiles):
                 weave_weight(raw, t, grp[:, i])
-            return quantise_woven(grp, name)
+            return quantise_woven(grp, name, "codes_" + name)
 
         def product(acc, wq, words, scales):
             nc.tensor.matmul_mx(out=acc, lhsT=wq[0].bitcast(FP8X4), lhsT_scale=wq[1], rhs=words.bitcast(FP8X4), rhs_scale=scales, start=True, stop=True)
@@ -233,16 +233,15 @@ def tile_picked_triosoftbmaxbhopp_none_p_kernel(tc, x_words, x_scales, w1, w2, w
         HALF = 2 * P
         grp4 = sb([P, NT, P, 4], BF16, "grp_w4")
         for t in range(NT):
+            weave_weight(raw4, t, grp4[:, t])
             low_side(0, t, sb([P, HALF], F32, "low%d" % t)[:])
             high_side(0, HALF, t, slot([P, HALF], F32, "high", "high%d" % t)[:])
-            weave_weight(raw4, t, grp4[:, t])
-        q4 = quantise_woven(grp4, "w4")
         low_side(1, 0, sb([P, HALF], F32, "low4")[:])
+        low_side(1, 1, sb([P, HALF], F32, "low5")[:])
         turn_back(0)
         turn_back(1)
-        mid = slot([P, S], F32, "gaps_mid", "high%d" % (NT - 1))
-        low_side(1, 1, mid[:, :HALF])
-        low_side(1, 2, mid[:, HALF:])
+        q4 = quantise_woven(grp4, "w4", "high%d" % (NT - 1))
+        low_side(1, 2, slot([P, HALF], F32, "low6", "zrow0")[:])
         last_product(0, HALF, [hacc[t][:, :HALF] for t in range(NT)])
         late = slot([P, HALF + 2 * S], F32, "gaps_late", "zg0")
         low_side(1, 3, late[:, :HALF])

@@ -14,10 +14,16 @@ ALU = mybir.AluOpType
 ACT = mybir.ActivationFunctionType
 
 P = 128
-K, T, S, N, H = 512, 2048, 512, 512, 512
-NT = 4
-NB = 4
-FLOPS = 4 * 2 * 512 * 512 * 512
+T = 2048
+S = 512
+F = 512
+PACK = 4
+ROW_TILES = F // P
+COL_BLOCKS = S // P
+HALF = S // 2
+LAST = ROW_TILES - 1
+PER_COLUMN = 16
+FLOPS = 4 * 2 * F * F * S
 
 
 def tile_picked_triosoftbmaxbhopp_none_p_kernel(tc, x_words, x_scales, w1, w2, w3, gn, w4, offs, two, three, n1, n2, n3, n4, n5, n6, out):
@@ -27,247 +33,243 @@ def tile_picked_triosoftbmaxbhopp_none_p_kernel(tc, x_words, x_scales, w1, w2, w
         keep = ctx.enter_context(tc.tile_pool(name="keep", bufs=1))
         psum = ctx.enter_context(tc.psum_pool(name="psum", bufs=1))
 
-        def load_list(src, name):
-            t = lists.tile([P, S // 16], U16, name=name)
-            nc.sync.dma_start(t[:], src)
-            return t
-
-        def sb(shape, dtype, name):
-            return keep.tile(shape, dtype, name=name, align_bytes=64)
-
-        x_sc = sb([P, T], U8, "x_sc")
-        nc.gpsimd.memset(x_sc[:].bitcast(I32), 0)
-
-        def load_weight(w, name):
-            raw = sb([P, 4, H], F32, name)
-            nc.sync.dma_start(raw[:], w.rearrange("(p j) c -> p j c", j=4))
-            return raw
-
-        l_two = load_list(two, "l_two")
-        l_offs = load_list(offs, "l_offs")
-        l_three = load_list(three, "l_three")
-        l_n2 = load_list(n2, "l_n2")
-        l_n1 = load_list(n1, "l_n1")
-        l_n3 = load_list(n3, "l_n3")
-        x_w = sb([P, T], U32, "x_w")
-        nc.sync.dma_start(x_w[:].bitcast(I32), x_words[0].rearrange("p n t -> p (n t)").bitcast(I32))
-        for q in range(4):
-            nc.sync.dma_start(x_sc[32 * q : 32 * q + 4, :].bitcast(I32), x_scales[0, 4 * q : 4 * q + 4, :].bitcast(I32))
-        l_n4 = load_list(n4, "l_n4")
-        l_n5 = load_list(n5, "l_n5")
-        raw2 = load_weight(w2, "raw2")
-        raw1 = load_weight(w1, "raw1")
-        gain = sb([P, 4], F32, "gain")
-        nc.sync.dma_start(gain[:], gn.rearrange("(p s) o -> p (s o)", s=4))
-        raw3 = load_weight(w3, "raw3")
-        raw4 = sb([P, 4, N], F32, "raw4")
-        w4_rows = w4.rearrange("(b t e) c -> t b e c", t=NT, e=8)
-        for t in range(NT):
-            nc.sync.dma_start(raw4[:, t, :], w4_rows[t])
-        l_n6 = load_list(n6, "l_n6")
-
-        warm = sb([P, 2], F32, "warm")
-        nc.gpsimd.memset(warm[:, 0:1], 0.0)
-        nc.scalar.activation(warm[:, 1:2], warm[:, 0:1], ACT.Sigmoid)
-
-        ident = sb([P, P], F32, "ident")
-        make_identity(nc, ident[:])
-        dwin = [sb([P, 2 * S], F32, "dwin%d" % t) for t in range(NT)]
-        for t in range(NT):
-            nc.vector.memset(dwin[t][:, S:], 0.0)
-
-        def pick_scales(lst, name, tag):
-            g = keep.tile([P, S], U8, name=name, tag=tag, align_bytes=64)
-            nc.vector.tensor_copy(g[:], x_sc[:].indirect(lst[:]))
-            return g
-
-        def pick_words(lst, name, tag):
-            g = keep.tile([P, S], U32, name=name, tag=tag, align_bytes=64)
-            nc.vector.tensor_copy(g[:], x_w[:].indirect(lst[:]))
-            return g
-
-        def weave_weight(raw, t, dst):
-            nc.scalar.copy(
-                dst.rearrange("p (b h i) j -> p b h j i", h=2, i=4),
-                raw[:].rearrange("p j (b t h i) -> p t b h j i", t=NT, h=2, i=4)[:, t],
-            )
-
-        def quantise_woven(grp, name, tag):
-            count = grp.shape[1]
-            codes = keep.tile([P, count * P], U32, name="codes_" + name, tag=tag, align_bytes=64)
-            scales = sb([P, count * P], U8, "scales_" + name)
-            nc.vector.quantize_mx(out=codes[:].bitcast(FP8X4), scales=scales[:], in_=grp[:].rearrange("p t c j -> p (t c j)"))
-            return [(codes[:, i * P : (i + 1) * P], scales[:, i * P : (i + 1) * P]) for i in range(count)]
-
-        def quantise_weight(raw, name, tiles):
-            name = "%s%d" % (name, tiles[0])
-            grp = keep.tile([P, len(tiles), P, 4], BF16, name="grp", tag="grp_" + name, align_bytes=64)
-            for i, t in enumerate(tiles):
-                weave_weight(raw, t, grp[:, i])
-            return quantise_woven(grp, name, "codes_" + name)
-
-        def product(acc, wq, words, scales):
-            nc.tensor.matmul_mx(out=acc, lhsT=wq[0].bitcast(FP8X4), lhsT_scale=wq[1], rhs=words.bitcast(FP8X4), rhs_scale=scales, start=True, stop=True)
+        def sb(shape, dtype, name, tag=None):
+            return keep.tile(shape, dtype, name=name, tag=tag or name, align_bytes=64)
 
         def bank(group, i):
             return psum.tile([P, S], F32, name="%s%d" % (group, i))
 
-        g_two = pick_words(l_two, "g_two", "g_two")
-        g_offs = pick_words(l_offs, "g_offs", "g_offs")
-        g_three = pick_words(l_three, "g_three", "g_three")
-        s_two = pick_scales(l_two, "s_two", "s_two")
-        q2 = quantise_weight(raw2, "w2", (0, 1)) + quantise_weight(raw2, "w2", (2, 3))
-        s_offs = pick_scales(l_offs, "s_offs", "grp_w20")
-        s_three = pick_scales(l_three, "s_three", "grp_w22")
+        def entries(lst, first, count):
+            return lst[:, first // PER_COLUMN : (first + count) // PER_COLUMN]
 
-        ywin = [sb([P, 2 * S], F32, "ywin%d" % t) for t in range(NT)]
-        mwin = [sb([P, 2 * S], F32, "mwin%d" % t) for t in range(NT)]
-        nb = [sb([P, S], F32, "nb%d" % t) for t in range(NT)]
+        def load_list(src, name):
+            lst = lists.tile([P, S // PER_COLUMN], U16, name=name)
+            nc.sync.dma_start(lst[:], src)
+            return lst
 
-        dacc = [bank("a", t) for t in range(NT)]
-        yacc = [bank("z", t) for t in range(NT)]
-        for t in range(NT):
-            product(dacc[t][:], q2[t], g_two[:], s_two[:])
+        def load_weight(w, name):
+            raw = sb([P, PACK, F], F32, name)
+            nc.sync.dma_start(raw[:], w.rearrange("(p j) c -> p j c", j=PACK))
+            return raw
 
-        def d_side(t):
-            nc.scalar.activation(ywin[t][:, S:], dacc[t][:], ACT.Tanh)
-            nc.scalar.copy(dwin[t][:, :S], dacc[t][:])
-            nc.vector.tensor_tensor(mwin[t][:, S:], dwin[t][:].indirect(l_n2[:]), ywin[t][:, S:], ALU.mult)
+        x_sc = sb([P, T], U8, "x_sc")
+        nc.vector.memset(x_sc[:].bitcast(I32), 0)
+        l_two = load_list(two, "l_two")
+        l_offs = load_list(offs, "l_offs")
+        x_w = sb([P, T], U32, "x_w")
+        nc.sync.dma_start(x_w[:].bitcast(I32), x_words[0].rearrange("p n t -> p (n t)").bitcast(I32))
+        for q in range(4):
+            nc.sync.dma_start(x_sc[32 * q : 32 * q + 4, :].bitcast(I32), x_scales[0, 4 * q : 4 * q + 4, :].bitcast(I32))
+        raw2 = load_weight(w2, "raw2")
+        l_three = load_list(three, "l_three")
+        l_n2 = load_list(n2, "l_n2")
+        raw1 = load_weight(w1, "raw1")
+        l_n1 = load_list(n1, "l_n1")
+        l_n3 = load_list(n3, "l_n3")
+        l_n4 = load_list(n4, "l_n4")
+        raw3 = load_weight(w3, "raw3")
+        gain = sb([P, PACK], F32, "gain")
+        nc.sync.dma_start(gain[:], gn.rearrange("(p j) o -> p (j o)", j=PACK))
+        raw4 = sb([P, PACK, F], F32, "raw4")
+        w4_rows = w4.rearrange("(b t e) c -> t b e c", t=PACK, e=8)
+        for t in range(PACK):
+            nc.sync.dma_start(raw4[:, t, :], w4_rows[t])
+        l_n5 = load_list(n5, "l_n5")
+        l_n6 = load_list(n6, "l_n6")
 
-        def y_side(t):
-            product(yacc[t][:], q1[t], g_offs[:], s_offs[:])
-            nc.scalar.copy(ywin[t][:, :S], yacc[t][:])
-            nc.vector.tensor_tensor(mwin[t][:, :S], ywin[t][:].indirect(l_n1[:]), mwin[t][:, S:], ALU.subtract)
+        origin = sb([P, 2], F32, "origin")
+        nc.gpsimd.memset(origin[:, 0:1], 0.0)
+        nc.scalar.activation(origin[:, 1:2], origin[:, 0:1], ACT.Sigmoid)
 
-        q1 = quantise_weight(raw1, "w1", (0, 1, 2, 3))
-        d_side(0)
-        for t in range(1, NT):
-            if t == NT - 1:
-                q3 = quantise_weight(raw3, "w3", (0, 1, 2, 3))
-            d_side(t)
-            y_side(t - 1)
-        y_side(NT - 1)
-        for t in range(NT):
-            acc = bank("a", t)
-            product(acc[:], q3[t], g_three[:], s_three[:])
-            nc.scalar.activation(nb[t][:], acc[:], ACT.Copy, scale=-1.0)
+        ident = sb([P, P], F32, "ident")
+        make_identity(nc, ident[:])
 
-        gps = bank("a", 0)
-        for j in range(4):
-            nc.tensor.transpose(gps[:, j * P : (j + 1) * P], gain[:, j : j + 1].to_broadcast([P, P]), ident[:])
-        gain_row = sb([P, 2, 256], F32, "gain_row")
-        for u in range(2):
+        d_win = [sb([P, 2 * S], F32, "d_win%d" % t) for t in range(ROW_TILES)]
+        for t in range(ROW_TILES):
+            nc.vector.memset(d_win[t][:, S:], 0.0)
+
+        def pick(table, dtype, lst, name, tag=None):
+            picked = sb([P, S], dtype, name, tag)
+            nc.vector.tensor_copy(picked[:], table[:].indirect(lst[:]))
+            return picked
+
+        def weave_weight(raw, t, dst):
             nc.scalar.copy(
-                gain_row[:, u, :].rearrange("p (b x j e) -> p b x j e", x=2, j=4, e=2),
-                gps[:].rearrange("p (j b u e x) -> p u b x j e", j=4, u=2, e=2, x=2)[:, u],
+                dst.rearrange("p (b h i) j -> p b h j i", h=2, i=4),
+                raw[:].rearrange("p j (b t h i) -> p t b h j i", t=ROW_TILES, h=2, i=4)[:, t],
             )
 
+        def quantise_woven(woven, name, codes_tag=None):
+            count = woven.shape[1]
+            codes = sb([P, count * P], U32, "codes_" + name, codes_tag)
+            scales = sb([P, count * P], U8, "scales_" + name)
+            nc.vector.quantize_mx(out=codes[:].bitcast(FP8X4), scales=scales[:], in_=woven[:].rearrange("p t c j -> p (t c j)"))
+            return [(codes[:, i * P : (i + 1) * P], scales[:, i * P : (i + 1) * P]) for i in range(count)]
 
-        zt = [bank("z", c) for c in range(NB)]
+        def quantise_weight(raw, name, tiles):
+            woven = sb([P, len(tiles), P, PACK], BF16, "woven_" + name)
+            for i, t in enumerate(tiles):
+                weave_weight(raw, t, woven[:, i])
+            return quantise_woven(woven, name)
+
+        def product(acc, weight, words, scales):
+            nc.tensor.matmul_mx(out=acc, lhsT=weight[0].bitcast(FP8X4), lhsT_scale=weight[1], rhs=words.bitcast(FP8X4), rhs_scale=scales, start=True, stop=True)
+
+        two_w = pick(x_w, U32, l_two, "two_w")
+        offs_w = pick(x_w, U32, l_offs, "offs_w")
+        two_sc = pick(x_sc, U8, l_two, "two_sc")
+        offs_sc = pick(x_sc, U8, l_offs, "offs_sc")
+        q2 = quantise_weight(raw2, "w2_low", (0, 1)) + quantise_weight(raw2, "w2_high", (2, 3))
+        three_w = pick(x_w, U32, l_three, "three_w", "woven_w2_low")
+        three_sc = pick(x_sc, U8, l_three, "three_sc", "woven_w2_high")
+
+        y_win = [sb([P, 2 * S], F32, "y_win%d" % t) for t in range(ROW_TILES)]
+        m_win = [sb([P, 2 * S], F32, "m_win%d" % t) for t in range(ROW_TILES)]
+        neg_b = [sb([P, S], F32, "neg_b%d" % t) for t in range(ROW_TILES)]
+        all_tiles = tuple(range(ROW_TILES))
+
+        d_acc = [bank("a", t) for t in range(ROW_TILES)]
+        y_acc = [bank("z", t) for t in range(ROW_TILES)]
+        for t in range(ROW_TILES):
+            product(d_acc[t][:], q2[t], two_w[:], two_sc[:])
+
+        def d_side(t):
+            nc.scalar.activation(y_win[t][:, S:], d_acc[t][:], ACT.Tanh)
+            nc.scalar.copy(d_win[t][:, :S], d_acc[t][:])
+            nc.vector.tensor_tensor(m_win[t][:, S:], d_win[t][:].indirect(l_n2[:]), y_win[t][:, S:], ALU.mult)
+
+        def y_side(t):
+            product(y_acc[t][:], q1[t], offs_w[:], offs_sc[:])
+            nc.scalar.copy(y_win[t][:, :S], y_acc[t][:])
+            nc.vector.tensor_tensor(m_win[t][:, :S], y_win[t][:].indirect(l_n1[:]), m_win[t][:, S:], ALU.subtract)
+
+        q1 = quantise_weight(raw1, "w1", all_tiles)
+        d_side(0)
+        for t in range(1, ROW_TILES):
+            if t == LAST:
+                q3 = quantise_weight(raw3, "w3", all_tiles)
+            d_side(t)
+            y_side(t - 1)
+        y_side(LAST)
+        for t in range(ROW_TILES):
+            b_acc = bank("a", t)
+            product(b_acc[:], q3[t], three_w[:], three_sc[:])
+            nc.scalar.activation(neg_b[t][:], b_acc[:], ACT.Copy, scale=-1.0)
+
+        gain_acc = bank("a", 0)
+        for j in range(PACK):
+            nc.tensor.transpose(gain_acc[:, j * P : (j + 1) * P], gain[:, j : j + 1].to_broadcast([P, P]), ident[:])
+        gain_row = sb([P, 2, 2 * P], F32, "gain_row")
+        for u in range(2):
+            nc.scalar.copy(
+                gain_row[:, u, :].rearrange("p (b x j e) -> p b x j e", x=2, j=PACK, e=2),
+                gain_acc[:].rearrange("p (j b u e x) -> p u b x j e", j=PACK, u=2, e=2, x=2)[:, u],
+            )
+
+        sums = [bank("z", c) for c in range(COL_BLOCKS)]
 
         def add_turned(src, c, t, start=False, stop=False):
-            nc.tensor.matmul(zt[c][:, t * P : (t + 1) * P], lhsT=src, rhs=ident[:], is_transpose=True, start=start, stop=stop)
+            nc.tensor.matmul(sums[c][:, t * P : (t + 1) * P], lhsT=src, rhs=ident[:], is_transpose=True, start=start, stop=stop)
 
-        for t in range(NT):
-            for c in range(NB):
-                add_turned(mwin[t][:, c * P : (c + 1) * P], c, t, start=(t == 0))
-        for t in range(NT):
-            for c in range(NB):
-                add_turned(nb[t][:, c * P : (c + 1) * P], c, t)
+        for t in range(ROW_TILES):
+            for c in range(COL_BLOCKS):
+                add_turned(m_win[t][:, c * P : (c + 1) * P], c, t, start=(t == 0))
+        for t in range(ROW_TILES):
+            for c in range(COL_BLOCKS):
+                add_turned(neg_b[t][:, c * P : (c + 1) * P], c, t)
 
+        def min_term(first, t, term):
+            nc.vector.tensor_tensor(term, m_win[t][:].indirect(entries(l_n3, first, HALF)), neg_b[t][:, first : first + HALF], ALU.add)
+            nc.scalar.activation(term, term, ACT.Relu, scale=-1.0)
+            for i in range(HALF // P):
+                add_turned(term[:, i * P : (i + 1) * P], first // P + i, t)
 
-        def slot(shape, dtype, name, tag):
-            return keep.tile(shape, dtype, name=name, tag=tag, align_bytes=64)
-
-        def low_side(half, t, gap):
-            c0 = half * 2 * P
-            nc.vector.tensor_tensor(gap, mwin[t][:].indirect(l_n3[:, c0 // 16 : (c0 + 2 * P) // 16]), nb[t][:, c0 : c0 + 2 * P], ALU.add)
-            nc.scalar.activation(gap, gap, ACT.Relu, scale=-1.0)
-            for i in range(2):
-                add_turned(gap[:, i * P : (i + 1) * P], 2 * half + i, t)
-
-        def high_side(c0, width, t, gap):
-            nc.vector.tensor_tensor(gap, nb[t][:].indirect(l_n4[:, c0 // 16 : (c0 + width) // 16]), mwin[t][:, c0 : c0 + width], ALU.add)
-            nc.scalar.activation(gap, gap, ACT.Relu, scale=-1.0)
+        def max_term(first, width, t, term):
+            nc.vector.tensor_tensor(term, neg_b[t][:].indirect(entries(l_n4, first, width)), m_win[t][:, first : first + width], ALU.add)
+            nc.scalar.activation(term, term, ACT.Relu, scale=-1.0)
             for i in range(width // P):
-                add_turned(gap[:, i * P : (i + 1) * P], c0 // P + i, t, stop=(t == NT - 1))
+                add_turned(term[:, i * P : (i + 1) * P], first // P + i, t, stop=(t == LAST))
 
-        zg = [slot([P, 2 * P, 4], BF16, "zg", "zg%d" % half) for half in range(2)]
+        z_woven = [sb([P, HALF, PACK], BF16, "z_woven%d" % half) for half in range(2)]
 
         def turn_back(c):
-            zrow = slot([P, 2, P, 2], BF16, "zrow", "zrow%d" % c)
+            z_pairs = sb([P, 2, P, 2], BF16, "z_pairs%d" % c)
             nc.vector.tensor_tensor(
-                zrow[:],
-                zt[c][:].rearrange("p (u e f) -> p u f e", u=2, e=2),
+                z_pairs[:],
+                sums[c][:].rearrange("p (u e f) -> p u f e", u=2, e=2),
                 gain_row[:].rearrange("p u (f e) -> p u f e", e=2),
                 ALU.mult,
             )
-            pairs = zrow[:].rearrange("p u f e -> p (u f e)").bitcast(F32)
+            pair_words = z_pairs[:].rearrange("p u f e -> p (u f e)").bitcast(F32)
             back = bank("z", c)
             for u in range(2):
-                nc.tensor.transpose(back[:, u * P : (u + 1) * P], pairs[:, u * P : (u + 1) * P], ident[:])
+                nc.tensor.transpose(back[:, u * P : (u + 1) * P], pair_words[:, u * P : (u + 1) * P], ident[:])
+            half, at = divmod(c * P, HALF)
             nc.scalar.copy(
-                zg[c // 2][:, c % 2 * P : (c % 2 + 1) * P, :].rearrange("p c t -> p (c t)").bitcast(F32).rearrange("p (c u) -> p c u", u=2),
+                z_woven[half][:, at : at + P, :].rearrange("p c t -> p (c t)").bitcast(F32).rearrange("p (c u) -> p c u", u=2),
                 back[:, : 2 * P].rearrange("p (u c) -> p c u", u=2),
             )
 
-        swin = [sb([P, 2 * S], F32, "swin%d" % t) for t in range(NT)]
-        hacc = [bank("a", t) for t in range(NT)]
+        st_win = [sb([P, 2 * S], F32, "st_win%d" % t) for t in range(ROW_TILES)]
+        h_acc = [bank("a", t) for t in range(ROW_TILES)]
 
-        def last_product(c0, width, accs):
-            zq = sb([P, width], U32, "zq%d" % c0)
-            zs = sb([P, width], U8, "zs%d" % c0)
-            src = zg[c0 // (2 * P)][:, c0 % (2 * P) : c0 % (2 * P) + width, :]
-            nc.vector.quantize_mx(out=zq[:].bitcast(FP8X4), scales=zs[:], in_=src.rearrange("p c t -> p (c t)"))
-            for t in range(NT):
-                product(accs[t], q4[t], zq[:], zs[:])
+        def last_product(first, width, accs):
+            codes = sb([P, width], U32, "z_codes%d" % first)
+            scales = sb([P, width], U8, "z_scales%d" % first)
+            half, at = divmod(first, HALF)
+            nc.vector.quantize_mx(out=codes[:].bitcast(FP8X4), scales=scales[:], in_=z_woven[half][:, at : at + width, :].rearrange("p c t -> p (c t)"))
+            for t in range(ROW_TILES):
+                product(accs[t], q4[t], codes[:], scales[:])
 
-        def leave_bank(t, c0, width, acc, by_dma):
-            cols = slice(c0, c0 + width)
-            nc.scalar.activation(dwin[t][:, cols], acc, ACT.Copy, scale=2.0)
-            if by_dma:
-                nc.sync.dma_start(swin[t][:, S + c0 : S + c0 + width], dwin[t][:, cols])
+        def leave_bank(t, first, width, acc, second_by_dma):
+            window = d_win[t][:, first : first + width]
+            plain = st_win[t][:, S + first : S + first + width]
+            nc.scalar.activation(window, acc, ACT.Copy, scale=2.0)
+            if second_by_dma:
+                nc.sync.dma_start(plain, window)
             else:
-                nc.scalar.activation(swin[t][:, S + c0 : S + c0 + width], acc, ACT.Copy, scale=2.0)
+                nc.scalar.activation(plain, acc, ACT.Copy, scale=2.0)
 
-        HALF = 2 * P
-        grp4 = sb([P, NT, P, 4], BF16, "grp_w4")
-        for t in range(NT):
-            weave_weight(raw4, t, grp4[:, t])
-            low_side(0, t, sb([P, HALF], F32, "low%d" % t)[:])
-            high_side(0, HALF, t, slot([P, HALF], F32, "high", "high%d" % t)[:])
-        low_side(1, 0, sb([P, HALF], F32, "low4")[:])
-        low_side(1, 1, sb([P, HALF], F32, "low5")[:])
+        woven4 = sb([P, ROW_TILES, P, PACK], BF16, "woven_w4")
+        for t in range(ROW_TILES):
+            weave_weight(raw4, t, woven4[:, t])
+            min_term(0, t, sb([P, HALF], F32, "min_low%d" % t)[:])
+            max_term(0, HALF, t, sb([P, HALF], F32, "max_low%d" % t)[:])
+        min_term(HALF, 0, sb([P, HALF], F32, "min_high0")[:])
+        min_term(HALF, 1, sb([P, HALF], F32, "min_high1")[:])
         turn_back(0)
         turn_back(1)
-        q4 = quantise_woven(grp4, "w4", "high%d" % (NT - 1))
-        low_side(1, 2, slot([P, HALF], F32, "low6", "zrow0")[:])
-        last_product(0, HALF, [hacc[t][:, :HALF] for t in range(NT)])
-        late = slot([P, HALF + 2 * S], F32, "gaps_late", "zg0")
-        low_side(1, 3, late[:, :HALF])
-        for t in range(NT):
-            leave_bank(t, 0, HALF, hacc[t][:, :HALF], True)
-        for c in (2, 3):
-            for t in range(NT):
-                at = HALF + (c - 2) * S + t * P
-                high_side(c * P, P, t, late[:, at : at + P])
-        turn_back(2)
-        turn_back(3)
-        last_product(2 * P, P, [hacc[t][:, 2 * P : 3 * P] for t in range(NT)])
-        leave_bank(0, 2 * P, P, hacc[0][:, 2 * P : 3 * P], False)
-        tail = bank("z", 0)
-        last_product(3 * P, P, [tail[:, :P]] + [hacc[t][:, 3 * P :] for t in range(1, NT)])
-        leave_bank(0, 3 * P, P, tail[:, :P], False)
-        for t in range(1, NT):
-            leave_bank(t, HALF, HALF, hacc[t][:, HALF:], False)
+        q4 = quantise_woven(woven4, "w4", "max_low%d" % LAST)
+        min_term(HALF, 2, sb([P, HALF], F32, "min_high2", "z_pairs0")[:])
+        last_product(0, HALF, [h_acc[t][:, :HALF] for t in range(ROW_TILES)])
+        late = sb([P, HALF + 2 * ROW_TILES * P], F32, "late_terms", "z_woven0")
+        min_term(HALF, LAST, late[:, :HALF])
+        for t in range(ROW_TILES):
+            leave_bank(t, 0, HALF, h_acc[t][:, :HALF], True)
 
-        out_rows = out.rearrange("(b t e) c -> t b e c", t=NT, e=8)
-        sig = [sb([P, S], F32, "sig%d" % t) for t in range(NT)]
-        pieces = [(t, 0, S) for t in range(NT - 1)] + [(NT - 1, 0, S // 2), (NT - 1, S // 2, S)]
-        for t in range(NT):
-            nc.vector.tensor_tensor(swin[t][:, :S], dwin[t][:].indirect(l_n5[:]), swin[t][:, S:], ALU.add)
-        for t, lo, hi in pieces:
-            nc.scalar.activation(sig[t][:, lo:hi], swin[t][:].indirect(l_n6[:, lo // 16 : hi // 16]), ACT.Sigmoid)
-            res = sb([P, hi - lo], F32, "res%d_%d" % (t, lo))
-            nc.vector.scalar_tensor_tensor(res[:], sig[t][:, lo:hi], 0.5, swin[t][:, lo:hi], ALU.subtract, ALU.mult)
-            nc.sync.dma_start(out_rows[t][:, :, lo:hi], res[:])
+        third, fourth = HALF, HALF + P
+        for i, first in enumerate((third, fourth)):
+            for t in range(ROW_TILES):
+                at = HALF + (i * ROW_TILES + t) * P
+                max_term(first, P, t, late[:, at : at + P])
+        turn_back(third // P)
+        turn_back(fourth // P)
+        last_product(third, P, [h_acc[t][:, third:fourth] for t in range(ROW_TILES)])
+        leave_bank(0, third, P, h_acc[0][:, third:fourth], False)
+        h_end = bank("z", 0)
+        last_product(fourth, P, [h_end[:, :P]] + [h_acc[t][:, fourth:] for t in range(1, ROW_TILES)])
+        leave_bank(0, fourth, P, h_end[:, :P], False)
+        for t in range(1, ROW_TILES):
+            leave_bank(t, HALF, HALF, h_acc[t][:, HALF:], False)
+
+        out_rows = out.rearrange("(b t e) c -> t b e c", t=ROW_TILES, e=8)
+        sig = [sb([P, S], F32, "sig%d" % t) for t in range(ROW_TILES)]
+        pieces = [(t, 0, S) for t in range(LAST)] + [(LAST, 0, HALF), (LAST, HALF, HALF)]
+        for t in range(ROW_TILES):
+            nc.vector.tensor_tensor(st_win[t][:, :S], d_win[t][:].indirect(l_n5[:]), st_win[t][:, S:], ALU.add)
+        for t, first, width in pieces:
+            cols = slice(first, first + width)
+            nc.scalar.activation(sig[t][:, cols], st_win[t][:].indirect(entries(l_n6, first, width)), ACT.Sigmoid)
+            res = sb([P, width], F32, "res%d_%d" % (t, first))
+            nc.vector.scalar_tensor_tensor(res[:], sig[t][:, cols], origin[:, 1:2], st_win[t][:, cols], ALU.subtract, ALU.mult)
+            nc.sync.dma_start(out_rows[t][:, :, cols], res[:])

from contextlib import ExitStack

import concourse.mybir as mybir
from concourse.masks import make_identity

F32 = mybir.dt.float32
BF16 = mybir.dt.bfloat16
I32 = mybir.dt.int32
U32 = mybir.dt.uint32
U16 = mybir.dt.uint16
U8 = mybir.dt.uint8
FP8X4 = mybir.dt.float8_e4m3fn_x4
ALU = mybir.AluOpType
ACT = mybir.ActivationFunctionType

P = 128
T = 2048
S = 512
F = 512
PACK = 4
ROW_TILES = F // P
COL_BLOCKS = S // P
HALF = S // 2
LAST = ROW_TILES - 1
PER_COLUMN = 16
FLOPS = 4 * 2 * F * F * S


def tile_picked_triosoftbmaxbhopp_none_p_kernel(tc, x_words, x_scales, w1, w2, w3, gn, w4, offs, two, three, n1, n2, n3, n4, n5, n6, out):
    nc = tc.nc
    with ExitStack() as ctx:
        lists = ctx.enter_context(tc.tile_pool(name="lists", bufs=1))
        keep = ctx.enter_context(tc.tile_pool(name="keep", bufs=1))
        psum = ctx.enter_context(tc.psum_pool(name="psum", bufs=1))

        def sb(shape, dtype, name, tag=None):
            return keep.tile(shape, dtype, name=name, tag=tag or name, align_bytes=64)

        def bank(group, i):
            return psum.tile([P, S], F32, name="%s%d" % (group, i))

        def entries(lst, first, count):
            return lst[:, first // PER_COLUMN : (first + count) // PER_COLUMN]

        def load_list(src, name):
            lst = lists.tile([P, S // PER_COLUMN], U16, name=name)
            nc.sync.dma_start(lst[:], src)
            return lst

        def load_weight(w, name):
            raw = sb([P, PACK, F], F32, name)
            nc.sync.dma_start(raw[:], w.rearrange("(p j) c -> p j c", j=PACK))
            return raw

        x_sc = sb([P, T], U8, "x_sc")
        nc.vector.memset(x_sc[:].bitcast(I32), 0)
        l_two = load_list(two, "l_two")
        l_offs = load_list(offs, "l_offs")
        x_w = sb([P, T], U32, "x_w")
        nc.sync.dma_start(x_w[:].bitcast(I32), x_words[0].rearrange("p n t -> p (n t)").bitcast(I32))
        for q in range(4):
            nc.sync.dma_start(x_sc[32 * q : 32 * q + 4, :].bitcast(I32), x_scales[0, 4 * q : 4 * q + 4, :].bitcast(I32))
        raw2 = load_weight(w2, "raw2")
        l_three = load_list(three, "l_three")
        l_n2 = load_list(n2, "l_n2")
        raw1 = load_weight(w1, "raw1")
        l_n1 = load_list(n1, "l_n1")
        l_n3 = load_list(n3, "l_n3")
        l_n4 = load_list(n4, "l_n4")
        raw3 = load_weight(w3, "raw3")
        gain = sb([P, PACK], F32, "gain")
        nc.sync.dma_start(gain[:], gn.rearrange("(p j) o -> p (j o)", j=PACK))
        raw4 = sb([P, PACK, F], F32, "raw4")
        w4_rows = w4.rearrange("(b t e) c -> t b e c", t=PACK, e=8)
        for t in range(PACK):
            nc.sync.dma_start(raw4[:, t, :], w4_rows[t])
        l_n5 = load_list(n5, "l_n5")
        l_n6 = load_list(n6, "l_n6")

        origin = sb([P, 2], F32, "origin")
        nc.gpsimd.memset(origin[:, 0:1], 0.0)
        nc.scalar.activation(origin[:, 1:2], origin[:, 0:1], ACT.Sigmoid)

        ident = sb([P, P], F32, "ident")
        make_identity(nc, ident[:])

        d_win = [sb([P, 2 * S], F32, "d_win%d" % t) for t in range(ROW_TILES)]
        for t in range(ROW_TILES):
            nc.vector.memset(d_win[t][:, S:], 0.0)

        def pick(table, dtype, lst, name, tag=None):
            picked = sb([P, S], dtype, name, tag)
            nc.vector.tensor_copy(picked[:], table[:].indirect(lst[:]))
            return picked

        def weave_weight(raw, t, dst):
            nc.scalar.copy(
                dst.rearrange("p (b h i) j -> p b h j i", h=2, i=4),
                raw[:].rearrange("p j (b t h i) -> p t b h j i", t=ROW_TILES, h=2, i=4)[:, t],
            )

        def quantise_woven(woven, name, codes_tag=None):
            count = woven.shape[1]
            codes = sb([P, count * P], U32, "codes_" + name, codes_tag)
            scales = sb([P, count * P], U8, "scales_" + name)
            nc.vector.quantize_mx(out=codes[:].bitcast(FP8X4), scales=scales[:], in_=woven[:].rearrange("p t c j -> p (t c j)"))
            return [(codes[:, i * P : (i + 1) * P], scales[:, i * P : (i + 1) * P]) for i in range(count)]

        def quantise_weight(raw, name, tiles):
            woven = sb([P, len(tiles), P, PACK], BF16, "woven_" + name)
            for i, t in enumerate(tiles):
                weave_weight(raw, t, woven[:, i])
            return quantise_woven(woven, name)

        def product(acc, weight, words, scales):
            nc.tensor.matmul_mx(out=acc, lhsT=weight[0].bitcast(FP8X4), lhsT_scale=weight[1], rhs=words.bitcast(FP8X4), rhs_scale=scales, start=True, stop=True)

        two_w = pick(x_w, U32, l_two, "two_w")
        offs_w = pick(x_w, U32, l_offs, "offs_w")
        two_sc = pick(x_sc, U8, l_two, "two_sc")
        offs_sc = pick(x_sc, U8, l_offs, "offs_sc")
        q2 = quantise_weight(raw2, "w2_low", (0, 1)) + quantise_weight(raw2, "w2_high", (2, 3))
        three_w = pick(x_w, U32, l_three, "three_w", "woven_w2_low")
        three_sc = pick(x_sc, U8, l_three, "three_sc", "woven_w2_high")

        y_win = [sb([P, 2 * S], F32, "y_win%d" % t) for t in range(ROW_TILES)]
        m_win = [sb([P, 2 * S], F32, "m_win%d" % t) for t in range(ROW_TILES)]
        neg_b = [sb([P, S], F32, "neg_b%d" % t) for t in range(ROW_TILES)]
        all_tiles = tuple(range(ROW_TILES))

        d_acc = [bank("a", t) for t in range(ROW_TILES)]
        y_acc = [bank("z", t) for t in range(ROW_TILES)]
        for t in range(ROW_TILES):
            product(d_acc[t][:], q2[t], two_w[:], two_sc[:])

        def d_side(t):
            nc.scalar.activation(y_win[t][:, S:], d_acc[t][:], ACT.Tanh)
            nc.scalar.copy(d_win[t][:, :S], d_acc[t][:])
            nc.vector.tensor_tensor(m_win[t][:, S:], d_win[t][:].indirect(l_n2[:]), y_win[t][:, S:], ALU.mult)

        def y_side(t):
            product(y_acc[t][:], q1[t], offs_w[:], offs_sc[:])
            nc.scalar.copy(y_win[t][:, :S], y_acc[t][:])
            nc.vector.tensor_tensor(m_win[t][:, :S], y_win[t][:].indirect(l_n1[:]), m_win[t][:, S:], ALU.subtract)

        q1 = quantise_weight(raw1, "w1", all_tiles)
        d_side(0)
        for t in range(1, ROW_TILES):
            if t == LAST:
                q3 = quantise_weight(raw3, "w3", all_tiles)
            d_side(t)
            y_side(t - 1)
        y_side(LAST)
        for t in range(ROW_TILES):
            b_acc = bank("a", t)
            product(b_acc[:], q3[t], three_w[:], three_sc[:])
            nc.scalar.activation(neg_b[t][:], b_acc[:], ACT.Copy, scale=-1.0)

        gain_acc = bank("a", 0)
        for j in range(PACK):
            nc.tensor.transpose(gain_acc[:, j * P : (j + 1) * P], gain[:, j : j + 1].to_broadcast([P, P]), ident[:])
        gain_row = sb([P, 2, 2 * P], F32, "gain_row")
        for u in range(2):
            nc.scalar.copy(
                gain_row[:, u, :].rearrange("p (b x j e) -> p b x j e", x=2, j=PACK, e=2),
                gain_acc[:].rearrange("p (j b u e x) -> p u b x j e", j=PACK, u=2, e=2, x=2)[:, u],
            )

        sums = [bank("z", c) for c in range(COL_BLOCKS)]

        def add_turned(src, c, t, start=False, stop=False):
            nc.tensor.matmul(sums[c][:, t * P : (t + 1) * P], lhsT=src, rhs=ident[:], is_transpose=True, start=start, stop=stop)

        for t in range(ROW_TILES):
            for c in range(COL_BLOCKS):
                add_turned(m_win[t][:, c * P : (c + 1) * P], c, t, start=(t == 0))
        for t in range(ROW_TILES):
            for c in range(COL_BLOCKS):
                add_turned(neg_b[t][:, c * P : (c + 1) * P], c, t)

        def min_term(first, t, term):
            nc.vector.tensor_tensor(term, m_win[t][:].indirect(entries(l_n3, first, HALF)), neg_b[t][:, first : first + HALF], ALU.add)
            nc.scalar.activation(term, term, ACT.Relu, scale=-1.0)
            for i in range(HALF // P):
                add_turned(term[:, i * P : (i + 1) * P], first // P + i, t)

        def max_term(first, width, t, term):
            nc.vector.tensor_tensor(term, neg_b[t][:].indirect(entries(l_n4, first, width)), m_win[t][:, first : first + width], ALU.add)
            nc.scalar.activation(term, term, ACT.Relu, scale=-1.0)
            for i in range(width // P):
                add_turned(term[:, i * P : (i + 1) * P], first // P + i, t, stop=(t == LAST))

        z_woven = [sb([P, HALF, PACK], BF16, "z_woven%d" % half) for half in range(2)]

        def turn_back(c):
            z_pairs = sb([P, 2, P, 2], BF16, "z_pairs%d" % c)
            nc.vector.tensor_tensor(
                z_pairs[:],
                sums[c][:].rearrange("p (u e f) -> p u f e", u=2, e=2),
                gain_row[:].rearrange("p u (f e) -> p u f e", e=2),
                ALU.mult,
            )
            pair_words = z_pairs[:].rearrange("p u f e -> p (u f e)").bitcast(F32)
            back = bank("z", c)
            for u in range(2):
                nc.tensor.transpose(back[:, u * P : (u + 1) * P], pair_words[:, u * P : (u + 1) * P], ident[:])
            half, at = divmod(c * P, HALF)
            nc.scalar.copy(
                z_woven[half][:, at : at + P, :].rearrange("p c t -> p (c t)").bitcast(F32).rearrange("p (c u) -> p c u", u=2),
                back[:, : 2 * P].rearrange("p (u c) -> p c u", u=2),
            )

        st_win = [sb([P, 2 * S], F32, "st_win%d" % t) for t in range(ROW_TILES)]
        h_acc = [bank("a", t) for t in range(ROW_TILES)]

        def last_product(first, width, accs):
            codes = sb([P, width], U32, "z_codes%d" % first)
            scales = sb([P, width], U8, "z_scales%d" % first)
            half, at = divmod(first, HALF)
            nc.vector.quantize_mx(out=codes[:].bitcast(FP8X4), scales=scales[:], in_=z_woven[half][:, at : at + width, :].rearrange("p c t -> p (c t)"))
            for t in range(ROW_TILES):
                product(accs[t], q4[t], codes[:], scales[:])

        def leave_bank(t, first, width, acc, second_by_dma):
            window = d_win[t][:, first : first + width]
            plain = st_win[t][:, S + first : S + first + width]
            nc.scalar.activation(window, acc, ACT.Copy, scale=2.0)
            if second_by_dma:
                nc.sync.dma_start(plain, window)
            else:
                nc.scalar.activation(plain, acc, ACT.Copy, scale=2.0)

        woven4 = sb([P, ROW_TILES, P, PACK], BF16, "woven_w4")
        for t in range(ROW_TILES):
            weave_weight(raw4, t, woven4[:, t])
            min_term(0, t, sb([P, HALF], F32, "min_low%d" % t)[:])
            max_term(0, HALF, t, sb([P, HALF], F32, "max_low%d" % t)[:])
        min_term(HALF, 0, sb([P, HALF], F32, "min_high0")[:])
        min_term(HALF, 1, sb([P, HALF], F32, "min_high1")[:])
        turn_back(0)
        turn_back(1)
        q4 = quantise_woven(woven4, "w4", "max_low%d" % LAST)
        min_term(HALF, 2, sb([P, HALF], F32, "min_high2", "z_pairs0")[:])
        last_product(0, HALF, [h_acc[t][:, :HALF] for t in range(ROW_TILES)])
        late = sb([P, HALF + 2 * ROW_TILES * P], F32, "late_terms", "z_woven0")
        min_term(HALF, LAST, late[:, :HALF])
        for t in range(ROW_TILES):
            leave_bank(t, 0, HALF, h_acc[t][:, :HALF], True)

        third, fourth = HALF, HALF + P
        for i, first in enumerate((third, fourth)):
            for t in range(ROW_TILES):
                at = HALF + (i * ROW_TILES + t) * P
                max_term(first, P, t, late[:, at : at + P])
        turn_back(third // P)
        turn_back(fourth // P)
        last_product(third, P, [h_acc[t][:, third:fourth] for t in range(ROW_TILES)])
        leave_bank(0, third, P, h_acc[0][:, third:fourth], False)
        h_end = bank("z", 0)
        last_product(fourth, P, [h_end[:, :P]] + [h_acc[t][:, fourth:] for t in range(1, ROW_TILES)])
        leave_bank(0, fourth, P, h_end[:, :P], False)
        for t in range(1, ROW_TILES):
            leave_bank(t, HALF, HALF, h_acc[t][:, HALF:], False)

        out_rows = out.rearrange("(b t e) c -> t b e c", t=ROW_TILES, e=8)
        sig = [sb([P, S], F32, "sig%d" % t) for t in range(ROW_TILES)]
        pieces = [(t, 0, S) for t in range(LAST)] + [(LAST, 0, HALF), (LAST, HALF, HALF)]
        for t in range(ROW_TILES):
            nc.vector.tensor_tensor(st_win[t][:, :S], d_win[t][:].indirect(l_n5[:]), st_win[t][:, S:], ALU.add)
        for t, first, width in pieces:
            cols = slice(first, first + width)
            nc.scalar.activation(sig[t][:, cols], st_win[t][:].indirect(entries(l_n6, first, width)), ACT.Sigmoid)
            res = sb([P, width], F32, "res%d_%d" % (t, first))
            nc.vector.scalar_tensor_tensor(res[:], sig[t][:, cols], origin[:, 1:2], st_win[t][:, cols], ALU.subtract, ALU.mult)
            nc.sync.dma_start(out_rows[t][:, :, cols], res[:])
